import numpy as np
import ml_dtypes


def mxq(x, axis, fmt="e4m3"):
    dtype, down = {"e4m3": (ml_dtypes.float8_e4m3fn, 7), "e5m2": (ml_dtypes.float8_e5m2, 14)}[fmt]
    v = np.moveaxis(np.asarray(x, np.float32).astype(ml_dtypes.bfloat16).astype(np.float64), axis, -1)
    blocks = v.reshape(v.shape[:-1] + (-1, 32))
    amax = np.abs(blocks).max(-1, keepdims=True)
    byte = np.maximum(np.where(amax > 0, np.frexp(amax)[1] - 1 + 127, 0) - down, 1)
    scale = np.exp2(byte - 127.0)
    codes = (blocks / scale).astype(np.float32).astype(dtype).astype(np.float64)
    return np.moveaxis((codes * scale).reshape(v.shape), -1, axis)


WIDE = False


def mx_kscale(k):
    if not WIDE:
        return np.ones(k)
    levels = np.array([10, -10, 5, -5, 0])
    if k % 512:
        return np.exp2(np.random.permutation(np.resize(levels, k // 32))).repeat(32)
    a = np.empty((k // 512, 16))
    for p in range(k // 512):
        a[p, :8] = np.random.permutation(np.resize(levels, 8))
        for g in range(8):
            far = levels[np.abs(levels - a[p, g]) >= 10]
            a[p, g + 8] = far[np.random.randint(len(far))]
    return np.exp2(a.ravel()).repeat(32)


def f64(x):
    return np.asarray(x).astype(np.float64)


def striped(idx):
    return np.tile(idx.reshape(-1, 16).T, (8, 1)).astype(np.uint16)


def unstriped(offs):
    return offs[:16].T.reshape(-1).astype(np.int64)


E2M1 = np.array([0.0, 0.5, 1.0, 1.5, 2.0, 3.0, 4.0, 6.0, -0.0, -0.5, -1.0, -1.5, -2.0, -3.0, -4.0, -6.0])


def pack_weight(w, fmt):
    k, n = w.shape
    w = f64(np.asarray(w, np.float32).astype(ml_dtypes.bfloat16)).reshape(k // 32, 32, n)
    amax = np.abs(w).max(1)
    if fmt == "e4m3":
        byte = np.frexp(amax)[1] - 1 + 127 - 7
    else:
        mant, ex = np.frexp(amax / 6.0)
        byte = np.where(mant > 0.5, ex, ex - 1) + 127
    byte = np.clip(np.where(amax > 0, byte, 1), 1, 254)
    scaled = (w * np.exp2(127.0 - byte)[:, None, :]).reshape(k, n).astype(np.float32)
    by_word = np.ascontiguousarray(scaled.reshape(k // 512, 128, 4, n).transpose(0, 1, 3, 2))
    if fmt == "e4m3":
        words = by_word.astype(ml_dtypes.float8_e4m3fn).view(np.uint8)
    else:
        c = by_word.astype(ml_dtypes.float4_e2m1fn).view(np.uint8) & 0xF
        words = (c[..., 0::2] | (c[..., 1::2] << 4)).reshape(k // 512, 128, 2 * n)
    return np.ascontiguousarray(words), np.ascontiguousarray(byte.astype(np.uint8).reshape(k // 512, 16, n))


def unpack_weight(words, scales, fmt):
    g, _, n = scales.shape
    words = np.ascontiguousarray(words).reshape(g, 128, n, -1)
    if fmt == "e4m3":
        vals = words.view(ml_dtypes.float8_e4m3fn).astype(np.float64)
    else:
        nib = np.empty((g, 128, n, 4), np.uint8)
        nib[..., 0::2] = words & 0xF
        nib[..., 1::2] = words >> 4
        vals = E2M1[nib]
    vals = vals * np.repeat(np.exp2(scales.astype(np.float64) - 127.0), 8, axis=1)[..., None]
    return vals.transpose(0, 1, 3, 2).reshape(g * 512, n)


def gelu(v):
    return 0.5 * v * (1.0 + np.tanh(np.sqrt(2.0 / np.pi) * (v + 0.044715 * v**3)))


K, T, S, H, K2, T3, P, N = 1024, 4096, 1024, 1024, 1536, 2048, 512, 512

def setup_inputs():
    n = np.random.standard_normal
    s = mx_kscale(K)[:, None]
    s2 = mx_kscale(K2)[:, None]
    u = mx_kscale(H)[:, None]
    tab_words, tab_scales = pack_weight(n((K, T)) * s, "e4m3")
    tab2_words, tab2_scales = pack_weight((n((K2, T3)) + 0.5) * s2, "e4m3")
    w1 = (1.2 * n((K, H)) / np.sqrt(K) / s).astype(np.float32)
    b1 = (0.5 * n(H)).astype(np.float32)
    gain = (u[:, 0] * np.exp(0.4 * n(H))).astype(np.float32)
    w2_words, w2_scales = pack_weight(1.15 * n((H, N)) / np.sqrt(H) / u, "e2m1")
    w3 = (0.52 * n((K2, N)) / np.sqrt(K2) / s2).astype(np.float32)
    w4_words, w4_scales = pack_weight((0.7 * n((K2, N)) / np.sqrt(K2) - 2.0 / K2) / s2, "e4m3")
    offs = striped(np.random.permutation(T)[:S])
    offs2 = striped(np.random.permutation(T3)[:P])
    pos1 = striped(np.random.permutation(S)[:P])
    return {"tab_words": tab_words, "tab_scales": tab_scales, "tab2_words": tab2_words, "tab2_scales": tab2_scales,
            "w1": w1, "b1": b1, "gain": gain, "w2_words": w2_words, "w2_scales": w2_scales,
            "w3": w3, "w4_words": w4_words, "w4_scales": w4_scales,
            "offs": offs, "offs2": offs2, "pos1": pos1}

def reference(tab_words, tab_scales, tab2_words, tab2_scales, w1, b1, gain, w2_words, w2_scales,
              w3, w4_words, w4_scales, offs, offs2, pos1):
    v = unpack_weight(tab_words, tab_scales, "e4m3")[:, unstriped(offs)]
    v2 = unpack_weight(tab2_words, tab2_scales, "e4m3")[:, unstriped(offs2)]
    x = mxq(f64(w1), 0, "e4m3").T @ v
    h = np.tanh(x + f64(b1)[:, None]) * f64(gain)[:, None]
    hq = mxq(h, 0, "e4m3")
    y = unpack_weight(w2_words, w2_scales, "e2m1").T @ hq
    d = mxq(f64(w3), 0, "e4m3").T @ v2
    e = unpack_weight(w4_words, w4_scales, "e4m3").T @ v2
    b = np.sin(d) + np.exp(e)
    return np.maximum(b, y[:, unstriped(pos1)])

@@ -1,0 +1,347 @@
+import math
+from contextlib import ExitStack
+
+import concourse.mybir as mybir
+
+
+K, T, S, H, K2, T3, NOTES, N = 1024, 4096, 1024, 1024, 1536, 2048, 512, 512
+FLOPS = 2 * K * H * S + 2 * H * N * S + 2 * 2 * K2 * N * NOTES
+
+F32 = mybir.dt.float32
+BF16 = mybir.dt.bfloat16
+I32 = mybir.dt.int32
+U32 = mybir.dt.uint32
+U16 = mybir.dt.uint16
+U8 = mybir.dt.uint8
+FP8X4 = mybir.dt.float8_e4m3fn_x4
+FP4X4 = mybir.dt.float4_e2m1fn_x4
+ACT = mybir.ActivationFunctionType
+ALU = mybir.AluOpType
+
+P = 128
+PACK = 4
+PASS = P * PACK
+BANK = 512
+QUADS = 4
+LIST_COLS = BANK // 16
+W3_PARTS = 2
+W3_COLS = N // W3_PARTS
+PIECE = BANK // 2
+
+
+def tile_list_dose_review_features_kernel(
+    tc, tab_words, tab_scales, tab2_words, tab2_scales, w1, b1, gain, w2_words, w2_scales,
+    w3, w4_words, w4_scales, offs, offs2, pos1, out,
+):
+    nc = tc.nc
+    k_passes, r_passes, m_passes = K // PASS, H // PASS, K2 // PASS
+    halves, n_tiles = S // BANK, N // P
+
+    with ExitStack() as ctx:
+        held = ctx.enter_context(tc.tile_pool(name="held", bufs=1))
+        ring = ctx.enter_context(tc.tile_pool(name="ring", bufs=1))
+        psum = ctx.enter_context(tc.psum_pool(name="psum", bufs=1))
+
+        def keep(shape, dtype, name):
+            return held.tile(shape, dtype, name=name, align_bytes=64)
+
+        def bank():
+            return psum.tile([P, BANK], F32, name="acc", bufs=8)
+
+        offs_t = held.tile([P, S // 16], U16, name="offs_t")
+        offs2_t = held.tile([P, NOTES // 16], U16, name="offs2_t")
+        pos_t = held.tile([P, NOTES // 16], U16, name="pos_t")
+        b1_t = keep([P, r_passes, PACK], F32, "b1_t")
+        gain_t = keep([P, r_passes, PACK], F32, "gain_t")
+        one = keep([P, 1], F32, "one")
+        eighth_pi = keep([P, 1], F32, "eighth_pi")
+
+        tab_w = [ring.tile([P, T], U32, name="wide", bufs=2, align_bytes=64) for a in range(k_passes)]
+        tab_s = keep([P, T], U8, "tab_s")
+        tab2_w = [keep([P, T3], U32, f"tab2_w{a}") for a in range(m_passes)]
+        tab2_s = keep([P, T3], U8, "tab2_s")
+        w2_w = keep([P, r_passes, 2 * N], U8, "w2_w")
+        w2_s = keep([P, r_passes, N], U8, "w2_s")
+        w4_w = keep([P, m_passes, N], U32, "w4_w")
+        w4_s = keep([P, N], U8, "w4_s")
+
+        nc.vector.memset(tab_s[:].bitcast(I32), 0)
+        nc.vector.memset(tab2_s[:].bitcast(I32), 0)
+        nc.vector.memset(w2_s[:].rearrange("p a n -> p (a n)").bitcast(I32), 0)
+        nc.vector.memset(w4_s[:].bitcast(I32), 0)
+        nc.vector.memset(one[:], 1.0)
+        nc.vector.tensor_scalar(eighth_pi[:], one[:], math.pi / 8, None, ALU.mult)
+
+        def load_packed_scales(tile, scales):
+            rows = PACK * scales.shape[0]
+            for q in range(QUADS):
+                nc.gpsimd.dma_start(
+                    out=tile[32 * q : 32 * q + rows, :].bitcast(I32),
+                    in_=scales[:, 4 * q : 4 * q + 4, :].bitcast(I32),
+                )
+
+        def load_w2_scales():
+            for q in range(QUADS):
+                nc.gpsimd.dma_start(
+                    out=w2_s[32 * q : 32 * q + 4, :, :].bitcast(I32),
+                    in_=w2_scales[:, 4 * q : 4 * q + 4, :].rearrange("a r n -> r a n").bitcast(I32),
+                )
+
+        def load_words(tile, words):
+            nc.sync.dma_start(out=tile[:].bitcast(I32), in_=words.rearrange("p t i -> p (t i)").bitcast(I32))
+
+        def load_rows(rows):
+            raw = ring.tile([P, PACK, rows.shape[1]], F32, name="raw%d" % rows.shape[1], bufs=(4 if rows.shape[1] == BANK else 6))
+            nc.sync.dma_start(out=raw[:], in_=rows.rearrange("(p j) c -> p j c", j=PACK))
+            return raw
+
+        def w1_rows(a, b):
+            return w1[a * PASS : (a + 1) * PASS, b * PASS : (b + 1) * PASS]
+
+        def mx_tiles(words, name):
+            return keep([P, words], U32, name + "_w"), keep([P, words], U8, name + "_s")
+
+        def quantise(rounded, target, first):
+            codes, scales = target
+            cols = slice(first, first + rounded.shape[1] // PACK)
+            nc.vector.quantize_mx(out=codes[:, cols].bitcast(FP8X4), scales=scales[:, cols], in_=rounded[:])
+
+        def piece_tile(tag):
+            return ring.tile([P, PIECE * PACK], BF16, name=tag, bufs=2, align_bytes=64)
+
+        def make_w1(raw, a, b, engines):
+            target = [mx_tiles(PIECE, f"w1q{a}{b}{u}") for u in range(2)]
+            pieces = []
+            for u in range(2):
+                rounded = piece_tile("by_" + engines[u])
+                dst = rounded[:].rearrange("p (t m j) -> p m j t", t=2, j=PACK)
+                src = raw[:].rearrange("p j (m t) -> p m j t", t=PACK)[:, :, :, 2 * u : 2 * u + 2]
+                if engines[u] == "S":
+                    nc.scalar.activation(dst, src, ACT.Copy)
+                else:
+                    nc.vector.tensor_copy(dst, src)
+                pieces.append(rounded)
+            for u in range(2):
+                quantise(pieces[u], target[u], 0)
+            w1q[a, b] = target
+
+        def round_w3(raw, eng):
+            rounded = ring.tile([P, W3_COLS * PACK], BF16, name="rounded3", bufs=6, align_bytes=64)
+            if eng == "G":
+                nc.gpsimd.tensor_scalar(
+                    rounded[:].rearrange("p (c j) -> p c j", j=PACK),
+                    raw[:].rearrange("p j c -> p c j"),
+                    1.0, 0.0, ALU.mult, ALU.add,
+                )
+                return rounded
+            dst = rounded[:].rearrange("p (c i j) -> p c j i", i=4, j=PACK)
+            src = raw[:].rearrange("p j (c i) -> p c j i", i=4)
+            if eng == "S":
+                nc.scalar.activation(dst, src, ACT.Copy)
+            else:
+                nc.vector.tensor_copy(dst, src)
+            return rounded
+
+        def gather(window, offsets, dtype, name):
+            if name.startswith("v_w") or name.startswith("picked"):
+                picked = ring.tile([P, BANK], dtype, name="four", bufs=4, align_bytes=64)
+            else:
+                picked = keep([P, BANK], dtype, name)
+            nc.vector.tensor_copy(picked[:], window[:].indirect(offsets))
+            return picked
+
+        def visit_list(half):
+            return offs_t[:, half * LIST_COLS : (half + 1) * LIST_COLS]
+
+        w1q, v_w, squashed, hq, w3q, w3r, w3raw = {}, {}, {}, {}, {}, {}, {}
+        y = {}
+        grown = [keep([P, NOTES], F32, f"grown{nt}") for nt in range(n_tiles)]
+        wave = [keep([P, NOTES], F32, f"wave{nt}") for nt in range(n_tiles)]
+        picked_y = {}
+
+        def first_stage(b, half):
+            squashed[b, half] = ring.tile([P, PACK, BANK], F32, name="squashed", bufs=3)
+            for t in range(PACK):
+                acc = bank()
+                cols = slice((t % 2) * P, (t % 2 + 1) * P)
+                for a in range(k_passes):
+                    codes, scales = w1q[a, b][t // 2]
+                    nc.tensor.matmul_mx(
+                        out=acc[:],
+                        lhsT=codes[:, cols].bitcast(FP8X4),
+                        lhsT_scale=scales[:, cols],
+                        rhs=v_w[a, half][:].bitcast(FP8X4),
+                        rhs_scale=v_s[half][4 * a : P, :],
+                        start=(a == 0),
+                        stop=(a == k_passes - 1),
+                    )
+                nc.scalar.activation(squashed[b, half][:, t, :], acc[:], ACT.Tanh, bias=b1_t[:, b, t : t + 1])
+
+        def make_h(b, half):
+            hq[b, half] = mx_tiles(BANK, f"hq{b}{half}")
+            pieces = []
+            for u in range(2):
+                rounded = piece_tile("by_V")
+                nc.vector.tensor_tensor(
+                    rounded[:].rearrange("p (c i t) -> p c t i", i=4, t=PACK),
+                    squashed[b, half][:, :, u * PIECE : (u + 1) * PIECE].rearrange("p t (c i) -> p c t i", i=4),
+                    gain_t[:, b, :].unsqueeze(1).unsqueeze(3).broadcast_to([P, PIECE // 4, PACK, 4]),
+                    ALU.mult,
+                )
+                pieces.append(rounded)
+            for u in range(2):
+                quantise(pieces[u], hq[b, half], u * PIECE)
+
+        def second_stage(half, nt, on_scalar):
+            if nt not in y:
+                pair = ring.tile([P, 2 * S], F32, name="wide", bufs=2, align_bytes=64)
+                y[nt], y[nt + 1] = pair[:, 0:S], pair[:, S : 2 * S]
+            acc = bank()
+            for b in reversed(range(r_passes)):
+                codes, scales = hq[b, half]
+                nc.tensor.matmul_mx(
+                    out=acc[:],
+                    lhsT=w2_w[:, b, 2 * P * nt : 2 * P * (nt + 1)].bitcast(FP4X4),
+                    lhsT_scale=w2_s[:, b, P * nt : P * (nt + 1)],
+                    rhs=codes[:].bitcast(FP8X4),
+                    rhs_scale=scales[:],
+                    start=(b == r_passes - 1),
+                    stop=(b == 0),
+                )
+            if on_scalar:
+                nc.scalar.activation(y[nt][:, half * BANK : (half + 1) * BANK], acc[:], ACT.Copy)
+            else:
+                nc.vector.tensor_copy(y[nt][:, half * BANK : (half + 1) * BANK], acc[:])
+
+        def exp_part(nt):
+            acc = bank()
+            cols = slice(nt * P, (nt + 1) * P)
+            for a in range(m_passes):
+                nc.tensor.matmul_mx(
+                    out=acc[:],
+                    lhsT=w4_w[:, a, cols].bitcast(FP8X4),
+                    lhsT_scale=w4_s[4 * a : P, cols],
+                    rhs=v2_w[a][:].bitcast(FP8X4),
+                    rhs_scale=v2_s[4 * a : P, :],
+                    start=(a == 0),
+                    stop=(a == m_passes - 1),
+                )
+            nc.scalar.activation(grown[nt][:], acc[:], ACT.Exp)
+
+        def sine_pair(pair):
+            for nt in pair:
+                acc = bank()
+                part, first = divmod(nt * P, W3_COLS)
+                cols = slice(first, first + P)
+                for a in range(m_passes):
+                    codes, scales = w3q[a, part]
+                    nc.tensor.matmul_mx(
+                        out=acc[:],
+                        lhsT=codes[:, cols].bitcast(FP8X4),
+                        lhsT_scale=scales[:, cols],
+                        rhs=v2_w[a][:].bitcast(FP8X4),
+                        rhs_scale=v2_s[4 * a : P, :],
+                        start=(a == 0),
+                        stop=(a == m_passes - 1),
+                    )
+                nc.scalar.activation(wave[nt][:], acc[:], ACT.Sin, bias=eighth_pi[:], scale=-0.25)
+            for nt in pair:
+                nc.scalar.activation(wave[nt][:], wave[nt][:], ACT.Square)
+            for nt in pair:
+                nc.scalar.activation(wave[nt][:], wave[nt][:], ACT.Square, bias=one[:], scale=-2.0)
+
+        def note_sum(nt):
+            nc.vector.scalar_tensor_tensor(grown[nt][:], wave[nt][:], 2.0, grown[nt][:], ALU.mult, ALU.add)
+
+        def pick(nt):
+            picked_y[nt] = gather(y[nt], pos_t[:], F32, f"picked_y{nt}")
+
+        def finish(nt):
+            nc.vector.scalar_tensor_tensor(picked_y[nt][:], grown[nt][:], -1.0, picked_y[nt][:], ALU.add, ALU.max)
+            nc.sync.dma_start(out=out[nt * P : (nt + 1) * P, :], in_=picked_y[nt][:])
+
+        def load_w3(part, a):
+            w3raw[a, part] = load_rows(w3[a * PASS : (a + 1) * PASS, part * W3_COLS : (part + 1) * W3_COLS])
+
+        def cast_w3(part, a, eng):
+            w3r[a, part] = round_w3(w3raw[a, part], eng)
+
+        def quant_w3(part, a):
+            w3q[a, part] = mx_tiles(W3_COLS, f"w3q{a}{part}")
+            quantise(w3r[a, part], w3q[a, part], 0)
+
+        load_packed_scales(tab_s, tab_scales)
+
+        load_packed_scales(tab2_s, tab2_scales)
+        load_w2_scales()
+        load_packed_scales(w4_s, w4_scales)
+
+        nc.sync.dma_start(offs_t[:], offs)
+        raw = load_rows(w1_rows(0, 0))
+        load_words(tab_w[0], tab_words[0])
+
+        make_w1(raw, 0, 0, "SS")
+        nc.sync.dma_start(offs2_t[:], offs2)
+        nc.sync.dma_start(out=b1_t[:], in_=b1.rearrange("(b p t) -> p b t", p=P, t=PACK))
+        nc.sync.dma_start(out=gain_t[:], in_=gain.rearrange("(b p t) -> p b t", p=P, t=PACK))
+        raw = load_rows(w1_rows(1, 0))
+        load_words(tab_w[1], tab_words[1])
+        v_s = [gather(tab_s, visit_list(half), U8, f"v_s{half}") for half in range(halves)]
+        for half in range(halves):
+            v_w[0, half] = gather(tab_w[0], visit_list(half), U32, f"v_w0{half}")
+
+        v2_s = gather(tab2_s, offs2_t[:], U8, "v2_s")
+        make_w1(raw, 1, 0, "SS")
+        for half in range(halves):
+            v_w[1, half] = gather(tab_w[1], visit_list(half), U32, f"v_w1{half}")
+        raws = [load_rows(w1_rows(a, 1)) for a in range(k_passes)]
+        nc.sync.dma_start(out=w2_w[:].bitcast(I32), in_=w2_words.rearrange("a p c -> p a c").bitcast(I32))
+        load_words(tab2_w[0], tab2_words[0])
+        load_words(tab2_w[1], tab2_words[1])
+        for a in range(m_passes):
+            load_w3(0, a)
+        load_words(tab2_w[2], tab2_words[2])
+        nc.sync.dma_start(out=w4_w[:].bitcast(I32), in_=w4_words.rearrange("a p c i -> p a (c i)").bitcast(I32))
+        nc.sync.dma_start(pos_t[:], pos1)
+        for a in range(m_passes):
+            load_w3(1, a)
+
+        first_stage(0, 0)
+        make_w1(raws[0], 0, 1, "VV")
+        first_stage(0, 1)
+        make_w1(raws[1], 1, 1, "VV")
+        make_h(0, 0)
+        first_stage(1, 0)
+        first_stage(1, 1)
+        make_h(1, 0)
+        for a in range(m_passes):
+            cast_w3(0, a, "SSS"[a])
+        for nt in range(n_tiles):
+            second_stage(0, nt, True)
+        v2_w = [gather(tab2_w[a], offs2_t[:], U32, f"v2_w{a}") for a in range(m_passes)]
+        for nt in range(n_tiles):
+            exp_part(nt)
+        for a in range(m_passes):
+            quant_w3(0, a)
+        sine_pair((0, 1))
+        make_h(0, 1)
+        make_h(1, 1)
+        for a in range(m_passes):
+            cast_w3(1, a, "VVV"[a])
+        for nt in range(n_tiles):
+            second_stage(1, nt, True)
+        for a in range(m_passes):
+            quant_w3(1, a)
+        sine_pair((2, 3))
+        note_sum(0)
+        note_sum(1)
+        pick(0)
+        pick(1)
+        pick(2)
+        pick(3)
+        finish(0)
+        finish(1)
+        note_sum(2)
+        note_sum(3)
+        finish(2)
+        finish(3)

@@ -2,6 +2,7 @@ import math
 from contextlib import ExitStack
 
 import concourse.mybir as mybir
+from concourse.masks import make_identity
 
 
 K, T, S, H, K2, T3, NOTES, N = 1024, 4096, 1024, 1024, 1536, 2048, 512, 512
@@ -27,6 +28,7 @@ LIST_COLS = BANK // 16
 W3_PARTS = 2
 W3_COLS = N // W3_PARTS
 PIECE = BANK // 2
+R3 = 3
 
 
 def tile_list_dose_review_features_kernel(
@@ -55,10 +57,11 @@ def tile_list_dose_review_features_kernel(
         gain_t = keep([P, r_passes, PACK], F32, "gain_t")
         one = keep([P, 1], F32, "one")
         eighth_pi = keep([P, 1], F32, "eighth_pi")
+        root_two = keep([P, 1], F32, "root_two")
 
         tab_w = [ring.tile([P, T], U32, name="wide", bufs=2, align_bytes=64) for a in range(k_passes)]
         tab_s = keep([P, T], U8, "tab_s")
-        tab2_w = [keep([P, T3], U32, f"tab2_w{a}") for a in range(m_passes)]
+        tab2_w = [ring.tile([P, T3], U32, name=f"tab2_w{a}", bufs=1, align_bytes=64) for a in range(m_passes)]
         tab2_s = keep([P, T3], U8, "tab2_s")
         w2_w = keep([P, r_passes, 2 * N], U8, "w2_w")
         w2_s = keep([P, r_passes, N], U8, "w2_s")
@@ -71,18 +74,19 @@ def tile_list_dose_review_features_kernel(
         nc.vector.memset(w4_s[:].bitcast(I32), 0)
         nc.vector.memset(one[:], 1.0)
         nc.vector.tensor_scalar(eighth_pi[:], one[:], math.pi / 8, None, ALU.mult)
+        nc.vector.tensor_scalar(root_two[:], one[:], math.sqrt(2.0), None, ALU.mult)
 
         def load_packed_scales(tile, scales):
             rows = PACK * scales.shape[0]
             for q in range(QUADS):
-                nc.gpsimd.dma_start(
+                nc.sync.dma_start(
                     out=tile[32 * q : 32 * q + rows, :].bitcast(I32),
                     in_=scales[:, 4 * q : 4 * q + 4, :].bitcast(I32),
                 )
 
         def load_w2_scales():
             for q in range(QUADS):
-                nc.gpsimd.dma_start(
+                nc.sync.dma_start(
                     out=w2_s[32 * q : 32 * q + 4, :, :].bitcast(I32),
                     in_=w2_scales[:, 4 * q : 4 * q + 4, :].rearrange("a r n -> r a n").bitcast(I32),
                 )
@@ -126,7 +130,7 @@ def tile_list_dose_review_features_kernel(
             w1q[a, b] = target
 
         def round_w3(raw, eng):
-            rounded = ring.tile([P, W3_COLS * PACK], BF16, name="rounded3", bufs=6, align_bytes=64)
+            rounded = ring.tile([P, W3_COLS * PACK], BF16, name="rounded3", bufs=R3, align_bytes=64)
             if eng == "G":
                 nc.gpsimd.tensor_scalar(
                     rounded[:].rearrange("p (c j) -> p c j", j=PACK),
@@ -177,11 +181,17 @@ def tile_list_dose_review_features_kernel(
                     )
                 nc.scalar.activation(squashed[b, half][:, t, :], acc[:], ACT.Tanh, bias=b1_t[:, b, t : t + 1])
 
-        def make_h(b, half):
+        def make_h(b, half, home):
+            whole = ring.tile([P, 2 * PIECE * PACK], BF16, name=home, bufs=1, align_bytes=64) if home.startswith("tab2") else None
             hq[b, half] = mx_tiles(BANK, f"hq{b}{half}")
             pieces = []
             for u in range(2):
-                rounded = piece_tile("by_V")
+                if whole is not None:
+                    rounded = whole[:, u * PIECE * PACK : (u + 1) * PIECE * PACK]
+                elif home == "rounded3":
+                    rounded = ring.tile([P, W3_COLS * PACK], BF16, name="rounded3", bufs=R3, align_bytes=64)
+                else:
+                    rounded = piece_tile("by_V")
                 nc.vector.tensor_tensor(
                     rounded[:].rearrange("p (c i t) -> p c t i", i=4, t=PACK),
                     squashed[b, half][:, :, u * PIECE : (u + 1) * PIECE].rearrange("p t (c i) -> p c t i", i=4),
@@ -213,51 +223,67 @@ def tile_list_dose_review_features_kernel(
             else:
                 nc.vector.tensor_copy(y[nt][:, half * BANK : (half + 1) * BANK], acc[:])
 
-        def exp_part(nt):
+        sums = {}
+
+        def exp_part(jt):
             acc = bank()
-            cols = slice(nt * P, (nt + 1) * P)
+            cols = slice(jt * P, (jt + 1) * P)
             for a in range(m_passes):
                 nc.tensor.matmul_mx(
                     out=acc[:],
-                    lhsT=w4_w[:, a, cols].bitcast(FP8X4),
-                    lhsT_scale=w4_s[4 * a : P, cols],
-                    rhs=v2_w[a][:].bitcast(FP8X4),
-                    rhs_scale=v2_s[4 * a : P, :],
+                    lhsT=v2_w[a][:, cols].bitcast(FP8X4),
+                    lhsT_scale=v2_s[4 * a : P, cols],
+                    rhs=w4_w[:, a, :].bitcast(FP8X4),
+                    rhs_scale=w4_s[4 * a : P, :],
                     start=(a == 0),
                     stop=(a == m_passes - 1),
                 )
-            nc.scalar.activation(grown[nt][:], acc[:], ACT.Exp)
+            nc.scalar.activation(grown[jt][:], acc[:], ACT.Exp)
 
         def sine_pair(pair):
-            for nt in pair:
+            part = pair[0] // 2
+            for slot in pair:
                 acc = bank()
-                part, first = divmod(nt * P, W3_COLS)
-                cols = slice(first, first + P)
-                for a in range(m_passes):
-                    codes, scales = w3q[a, part]
-                    nc.tensor.matmul_mx(
-                        out=acc[:],
-                        lhsT=codes[:, cols].bitcast(FP8X4),
-                        lhsT_scale=scales[:, cols],
-                        rhs=v2_w[a][:].bitcast(FP8X4),
-                        rhs_scale=v2_s[4 * a : P, :],
-                        start=(a == 0),
-                        stop=(a == m_passes - 1),
-                    )
-                nc.scalar.activation(wave[nt][:], acc[:], ACT.Sin, bias=eighth_pi[:], scale=-0.25)
-            for nt in pair:
-                nc.scalar.activation(wave[nt][:], wave[nt][:], ACT.Square)
-            for nt in pair:
-                nc.scalar.activation(wave[nt][:], wave[nt][:], ACT.Square, bias=one[:], scale=-2.0)
+                for side in range(2):
+                    jt = 2 * (slot % 2) + side
+                    cols = slice(jt * P, (jt + 1) * P)
+                    for a in range(m_passes):
+                        codes, scales = w3q[a, part]
+                        nc.tensor.matmul_mx(
+                            out=acc[:, side * W3_COLS : (side + 1) * W3_COLS],
+                            lhsT=v2_w[a][:, cols].bitcast(FP8X4),
+                            lhsT_scale=v2_s[4 * a : P, cols],
+                            rhs=codes[:].bitcast(FP8X4),
+                            rhs_scale=scales[:],
+                            start=(a == 0),
+                            stop=(a == m_passes - 1),
+                        )
+                nc.scalar.activation(wave[slot][:], acc[:], ACT.Sin, bias=eighth_pi[:], scale=-0.25)
+            for slot in pair:
+                nc.scalar.activation(wave[slot][:], wave[slot][:], ACT.Square)
+            for slot in pair:
+                nc.scalar.activation(
+                    wave[slot][:], wave[slot][:], ACT.Square, bias=root_two[:], scale=-2.0 * math.sqrt(2.0)
+                )
 
         def note_sum(nt):
-            nc.vector.scalar_tensor_tensor(grown[nt][:], wave[nt][:], 2.0, grown[nt][:], ALU.mult, ALU.add)
+            sums[nt] = bank()
+            part, first = divmod(nt * P, W3_COLS)
+            for jt in range(NOTES // P):
+                dst = sums[nt][:, jt * P : (jt + 1) * P]
+                at = (jt % 2) * W3_COLS + first
+                nc.tensor.matmul(
+                    dst, grown[jt][:, nt * P : (nt + 1) * P], identity[:], is_transpose=True, start=True, stop=False
+                )
+                nc.tensor.matmul(
+                    dst, wave[2 * part + jt // 2][:, at : at + P], identity[:], is_transpose=True, start=False, stop=True
+                )
 
         def pick(nt):
             picked_y[nt] = gather(y[nt], pos_t[:], F32, f"picked_y{nt}")
 
         def finish(nt):
-            nc.vector.scalar_tensor_tensor(picked_y[nt][:], grown[nt][:], -1.0, picked_y[nt][:], ALU.add, ALU.max)
+            nc.vector.scalar_tensor_tensor(picked_y[nt][:], sums[nt][:], -1.0, picked_y[nt][:], ALU.add, ALU.max)
             nc.sync.dma_start(out=out[nt * P : (nt + 1) * P, :], in_=picked_y[nt][:])
 
         def load_w3(part, a):
@@ -270,39 +296,39 @@ def tile_list_dose_review_features_kernel(
             w3q[a, part] = mx_tiles(W3_COLS, f"w3q{a}{part}")
             quantise(w3r[a, part], w3q[a, part], 0)
 
-        load_packed_scales(tab_s, tab_scales)
 
-        load_packed_scales(tab2_s, tab2_scales)
-        load_w2_scales()
-        load_packed_scales(w4_s, w4_scales)
-
-        nc.sync.dma_start(offs_t[:], offs)
+        identity = keep([P, P], F32, "identity")
+        make_identity(nc, identity[:])
         raw = load_rows(w1_rows(0, 0))
+        nc.sync.dma_start(offs_t[:], offs)
         load_words(tab_w[0], tab_words[0])
-
         make_w1(raw, 0, 0, "SS")
-        nc.sync.dma_start(offs2_t[:], offs2)
-        nc.sync.dma_start(out=b1_t[:], in_=b1.rearrange("(b p t) -> p b t", p=P, t=PACK))
-        nc.sync.dma_start(out=gain_t[:], in_=gain.rearrange("(b p t) -> p b t", p=P, t=PACK))
+
+        load_packed_scales(tab_s, tab_scales)
         raw = load_rows(w1_rows(1, 0))
         load_words(tab_w[1], tab_words[1])
-        v_s = [gather(tab_s, visit_list(half), U8, f"v_s{half}") for half in range(halves)]
+        nc.sync.dma_start(out=b1_t[:], in_=b1.rearrange("(b p t) -> p b t", p=P, t=PACK))
+        nc.sync.dma_start(out=gain_t[:], in_=gain.rearrange("(b p t) -> p b t", p=P, t=PACK))
         for half in range(halves):
             v_w[0, half] = gather(tab_w[0], visit_list(half), U32, f"v_w0{half}")
+        v_s = [gather(tab_s, visit_list(half), U8, f"v_s{half}") for half in range(halves)]
 
-        v2_s = gather(tab2_s, offs2_t[:], U8, "v2_s")
         make_w1(raw, 1, 0, "SS")
         for half in range(halves):
             v_w[1, half] = gather(tab_w[1], visit_list(half), U32, f"v_w1{half}")
         raws = [load_rows(w1_rows(a, 1)) for a in range(k_passes)]
         nc.sync.dma_start(out=w2_w[:].bitcast(I32), in_=w2_words.rearrange("a p c -> p a c").bitcast(I32))
+        nc.sync.dma_start(offs2_t[:], offs2)
         load_words(tab2_w[0], tab2_words[0])
+        load_packed_scales(tab2_s, tab2_scales)
         load_words(tab2_w[1], tab2_words[1])
-        for a in range(m_passes):
-            load_w3(0, a)
+        load_w2_scales()
         load_words(tab2_w[2], tab2_words[2])
+        load_packed_scales(w4_s, w4_scales)
         nc.sync.dma_start(out=w4_w[:].bitcast(I32), in_=w4_words.rearrange("a p c i -> p a (c i)").bitcast(I32))
         nc.sync.dma_start(pos_t[:], pos1)
+        for a in range(m_passes):
+            load_w3(0, a)
         for a in range(m_passes):
             load_w3(1, a)
 
@@ -310,26 +336,27 @@ def tile_list_dose_review_features_kernel(
         make_w1(raws[0], 0, 1, "VV")
         first_stage(0, 1)
         make_w1(raws[1], 1, 1, "VV")
-        make_h(0, 0)
+        make_h(0, 0, "by_V")
         first_stage(1, 0)
         first_stage(1, 1)
-        make_h(1, 0)
-        for a in range(m_passes):
-            cast_w3(0, a, "SSS"[a])
+        make_h(1, 0, "by_V")
         for nt in range(n_tiles):
             second_stage(0, nt, True)
+        v2_s = gather(tab2_s, offs2_t[:], U8, "v2_s")
         v2_w = [gather(tab2_w[a], offs2_t[:], U32, f"v2_w{a}") for a in range(m_passes)]
         for nt in range(n_tiles):
             exp_part(nt)
         for a in range(m_passes):
-            quant_w3(0, a)
-        sine_pair((0, 1))
-        make_h(0, 1)
-        make_h(1, 1)
+            cast_w3(0, a, "SVV"[a])
+        make_h(0, 1, "tab2_w2")
         for a in range(m_passes):
-            cast_w3(1, a, "VVV"[a])
+            quant_w3(0, a)
+        make_h(1, 1, "rounded3")
+        sine_pair((0, 1))
         for nt in range(n_tiles):
             second_stage(1, nt, True)
+        for a in range(m_passes):
+            cast_w3(1, a, "VVV"[a])
         for a in range(m_passes):
             quant_w3(1, a)
         sine_pair((2, 3))
@@ -337,10 +364,10 @@ def tile_list_dose_review_features_kernel(
         note_sum(1)
         pick(0)
         pick(1)
-        pick(2)
-        pick(3)
         finish(0)
         finish(1)
+        pick(2)
+        pick(3)
         note_sum(2)
         note_sum(3)
         finish(2)

@@ -4,7 +4,6 @@ from contextlib import ExitStack
 import concourse.mybir as mybir
 from concourse.masks import make_identity
 
-
 K, T, S, H, K2, T3, NOTES, N = 1024, 4096, 1024, 1024, 1536, 2048, 512, 512
 FLOPS = 2 * K * H * S + 2 * H * N * S + 2 * 2 * K2 * N * NOTES
 
@@ -24,11 +23,9 @@ PACK = 4
 PASS = P * PACK
 BANK = 512
 QUADS = 4
-LIST_COLS = BANK // 16
-W3_PARTS = 2
-W3_COLS = N // W3_PARTS
+LINE = 4
 PIECE = BANK // 2
-R3 = 3
+W3_PARTS = N // PIECE
 
 
 def tile_list_dose_review_features_kernel(
@@ -37,31 +34,31 @@ def tile_list_dose_review_features_kernel(
 ):
     nc = tc.nc
     k_passes, r_passes, m_passes = K // PASS, H // PASS, K2 // PASS
-    halves, n_tiles = S // BANK, N // P
+    halves, n_tiles, j_tiles = S // BANK, N // P, NOTES // P
 
     with ExitStack() as ctx:
         held = ctx.enter_context(tc.tile_pool(name="held", bufs=1))
         ring = ctx.enter_context(tc.tile_pool(name="ring", bufs=1))
-        psum = ctx.enter_context(tc.psum_pool(name="psum", bufs=1))
+        psum = ctx.enter_context(tc.psum_pool(name="psum", bufs=8))
 
         def keep(shape, dtype, name):
             return held.tile(shape, dtype, name=name, align_bytes=64)
 
+        def share(shape, dtype, tag, bufs):
+            return ring.tile(shape, dtype, name=tag, bufs=bufs, align_bytes=64)
+
         def bank():
-            return psum.tile([P, BANK], F32, name="acc", bufs=8)
+            return psum.tile([P, BANK], F32, name="bank")
 
         offs_t = held.tile([P, S // 16], U16, name="offs_t")
         offs2_t = held.tile([P, NOTES // 16], U16, name="offs2_t")
         pos_t = held.tile([P, NOTES // 16], U16, name="pos_t")
-        b1_t = keep([P, r_passes, PACK], F32, "b1_t")
-        gain_t = keep([P, r_passes, PACK], F32, "gain_t")
-        one = keep([P, 1], F32, "one")
-        eighth_pi = keep([P, 1], F32, "eighth_pi")
-        root_two = keep([P, 1], F32, "root_two")
-
-        tab_w = [ring.tile([P, T], U32, name="wide", bufs=2, align_bytes=64) for a in range(k_passes)]
+        vector_rows = keep([P, PASS], F32, "vector_rows")
+        per_row = keep([P, 2 * r_passes, PACK], F32, "per_row")
+        b1_t, gain_t = per_row[:, 0:r_passes, :], per_row[:, r_passes : 2 * r_passes, :]
+        tab_w = [share([P, T], U32, "wide", 2) for a in range(k_passes)]
         tab_s = keep([P, T], U8, "tab_s")
-        tab2_w = [ring.tile([P, T3], U32, name=f"tab2_w{a}", bufs=1, align_bytes=64) for a in range(m_passes)]
+        tab2_w = [share([P, T3], U32, f"tab2_w{a}", 1) for a in range(m_passes)]
         tab2_s = keep([P, T3], U8, "tab2_s")
         w2_w = keep([P, r_passes, 2 * N], U8, "w2_w")
         w2_s = keep([P, r_passes, N], U8, "w2_s")
@@ -69,15 +66,25 @@ def tile_list_dose_review_features_kernel(
         w4_s = keep([P, N], U8, "w4_s")
 
         nc.vector.memset(tab_s[:].bitcast(I32), 0)
+        nc.vector.memset(vector_rows[:], 0.0)
         nc.vector.memset(tab2_s[:].bitcast(I32), 0)
         nc.vector.memset(w2_s[:].rearrange("p a n -> p (a n)").bitcast(I32), 0)
         nc.vector.memset(w4_s[:].bitcast(I32), 0)
+
+        one = keep([P, 1], F32, "one")
+        eighth_pi = keep([P, 1], F32, "eighth_pi")
+        root_two = keep([P, 1], F32, "root_two")
         nc.vector.memset(one[:], 1.0)
         nc.vector.tensor_scalar(eighth_pi[:], one[:], math.pi / 8, None, ALU.mult)
         nc.vector.tensor_scalar(root_two[:], one[:], math.sqrt(2.0), None, ALU.mult)
+        identity = keep([P, P], F32, "identity")
+        make_identity(nc, identity[:])
+
+        def load_words(tile, words):
+            nc.sync.dma_start(out=tile[:].bitcast(I32), in_=words.rearrange("p t i -> p (t i)").bitcast(I32))
 
         def load_packed_scales(tile, scales):
-            rows = PACK * scales.shape[0]
+            rows = 4 * scales.shape[0]
             for q in range(QUADS):
                 nc.sync.dma_start(
                     out=tile[32 * q : 32 * q + rows, :].bitcast(I32),
@@ -91,80 +98,58 @@ def tile_list_dose_review_features_kernel(
                     in_=w2_scales[:, 4 * q : 4 * q + 4, :].rearrange("a r n -> r a n").bitcast(I32),
                 )
 
-        def load_words(tile, words):
-            nc.sync.dma_start(out=tile[:].bitcast(I32), in_=words.rearrange("p t i -> p (t i)").bitcast(I32))
-
-        def load_rows(rows):
-            raw = ring.tile([P, PACK, rows.shape[1]], F32, name="raw%d" % rows.shape[1], bufs=(4 if rows.shape[1] == BANK else 6))
-            nc.sync.dma_start(out=raw[:], in_=rows.rearrange("(p j) c -> p j c", j=PACK))
+        def load_rows(rows, tag, bufs):
+            raw = ring.tile([P, PACK, rows.shape[1]], F32, name=tag, bufs=bufs)
+            nc.sync.dma_start(out=raw[:], in_=rows.rearrange("(p i) c -> p i c", i=PACK))
             return raw
 
-        def w1_rows(a, b):
-            return w1[a * PASS : (a + 1) * PASS, b * PASS : (b + 1) * PASS]
+        def load_w1(a, b):
+            rows = w1[a * PASS : (a + 1) * PASS, b * PASS : (b + 1) * PASS]
+            return load_rows(rows, "w1_raw", k_passes * r_passes)
+
+        def load_w3(a, part):
+            rows = w3[a * PASS : (a + 1) * PASS, part * PIECE : (part + 1) * PIECE]
+            return load_rows(rows, "w3_raw", m_passes * W3_PARTS)
 
         def mx_tiles(words, name):
             return keep([P, words], U32, name + "_w"), keep([P, words], U8, name + "_s")
 
-        def quantise(rounded, target, first):
-            codes, scales = target
-            cols = slice(first, first + rounded.shape[1] // PACK)
-            nc.vector.quantize_mx(out=codes[:, cols].bitcast(FP8X4), scales=scales[:, cols], in_=rounded[:])
-
-        def piece_tile(tag):
-            return ring.tile([P, PIECE * PACK], BF16, name=tag, bufs=2, align_bytes=64)
-
-        def make_w1(raw, a, b, engines):
-            target = [mx_tiles(PIECE, f"w1q{a}{b}{u}") for u in range(2)]
-            pieces = []
-            for u in range(2):
-                rounded = piece_tile("by_" + engines[u])
-                dst = rounded[:].rearrange("p (t m j) -> p m j t", t=2, j=PACK)
-                src = raw[:].rearrange("p j (m t) -> p m j t", t=PACK)[:, :, :, 2 * u : 2 * u + 2]
-                if engines[u] == "S":
-                    nc.scalar.activation(dst, src, ACT.Copy)
-                else:
-                    nc.vector.tensor_copy(dst, src)
-                pieces.append(rounded)
-            for u in range(2):
-                quantise(pieces[u], target[u], 0)
-            w1q[a, b] = target
-
-        def round_w3(raw, eng):
-            rounded = ring.tile([P, W3_COLS * PACK], BF16, name="rounded3", bufs=R3, align_bytes=64)
-            if eng == "G":
-                nc.gpsimd.tensor_scalar(
-                    rounded[:].rearrange("p (c j) -> p c j", j=PACK),
-                    raw[:].rearrange("p j c -> p c j"),
-                    1.0, 0.0, ALU.mult, ALU.add,
-                )
-                return rounded
-            dst = rounded[:].rearrange("p (c i j) -> p c j i", i=4, j=PACK)
-            src = raw[:].rearrange("p j (c i) -> p c j i", i=4)
-            if eng == "S":
+        def round_on(engine, dst, src):
+            if engine is nc.scalar:
                 nc.scalar.activation(dst, src, ACT.Copy)
             else:
                 nc.vector.tensor_copy(dst, src)
-            return rounded
 
-        def gather(window, offsets, dtype, name):
-            if name.startswith("v_w") or name.startswith("picked"):
-                picked = ring.tile([P, BANK], dtype, name="four", bufs=4, align_bytes=64)
-            else:
-                picked = keep([P, BANK], dtype, name)
-            nc.vector.tensor_copy(picked[:], window[:].indirect(offsets))
+        def quantise(rounded, target, first):
+            codes, scales = target
+            cols = slice(first, first + PIECE)
+            nc.vector.quantize_mx(out=codes[:, cols].bitcast(FP8X4), scales=scales[:, cols], in_=rounded)
+
+        def gather(picked, window, offsets):
+            nc.vector.tensor_copy(picked[:], window.indirect(offsets))
             return picked
 
         def visit_list(half):
-            return offs_t[:, half * LIST_COLS : (half + 1) * LIST_COLS]
+            return offs_t[:, half * (BANK // 16) : (half + 1) * (BANK // 16)]
 
-        w1q, v_w, squashed, hq, w3q, w3r, w3raw = {}, {}, {}, {}, {}, {}, {}
-        y = {}
-        grown = [keep([P, NOTES], F32, f"grown{nt}") for nt in range(n_tiles)]
-        wave = [keep([P, NOTES], F32, f"wave{nt}") for nt in range(n_tiles)]
-        picked_y = {}
+        w1q, v_w, squashed, scaled, hq, w3r, w3q, y, sums, picked_y = {}, {}, {}, {}, {}, {}, {}, {}, {}, {}
+
+        def make_w1(raw, a, b, engine, tag):
+            w1q[a, b] = [mx_tiles(PIECE, f"w1q{a}{b}{u}") for u in range(2)]
+            pieces = []
+            for u in range(2):
+                rounded = share([P, PIECE * PACK], BF16, tag, 2)
+                round_on(
+                    engine,
+                    rounded[:].rearrange("p (t m i) -> p m i t", t=2, i=PACK),
+                    raw[:].rearrange("p i (m t) -> p m i t", t=PACK)[:, :, :, 2 * u : 2 * u + 2],
+                )
+                pieces.append(rounded)
+            for u in range(2):
+                quantise(pieces[u][:], w1q[a, b][u], 0)
 
         def first_stage(b, half):
-            squashed[b, half] = ring.tile([P, PACK, BANK], F32, name="squashed", bufs=3)
+            squashed[b, half] = share([P, PACK, BANK], F32, f"squashed{b}{half}", 1)
             for t in range(PACK):
                 acc = bank()
                 cols = slice((t % 2) * P, (t % 2 + 1) * P)
@@ -181,142 +166,157 @@ def tile_list_dose_review_features_kernel(
                     )
                 nc.scalar.activation(squashed[b, half][:, t, :], acc[:], ACT.Tanh, bias=b1_t[:, b, t : t + 1])
 
-        def make_h(b, half, home):
-            whole = ring.tile([P, 2 * PIECE * PACK], BF16, name=home, bufs=1, align_bytes=64) if home.startswith("tab2") else None
+        def by_lines(planes, u):
+            return planes[:, :, u * PIECE : (u + 1) * PIECE].rearrange("p t (c l) -> p c t l", l=LINE)
+
+        def as_words(rounded):
+            return rounded.rearrange("p (c l t) -> p c t l", l=LINE, t=PACK)
+
+        def quantise_h(b, half, pieces):
             hq[b, half] = mx_tiles(BANK, f"hq{b}{half}")
-            pieces = []
-            for u in range(2):
-                if whole is not None:
-                    rounded = whole[:, u * PIECE * PACK : (u + 1) * PIECE * PACK]
-                elif home == "rounded3":
-                    rounded = ring.tile([P, W3_COLS * PACK], BF16, name="rounded3", bufs=R3, align_bytes=64)
-                else:
-                    rounded = piece_tile("by_V")
-                nc.vector.tensor_tensor(
-                    rounded[:].rearrange("p (c i t) -> p c t i", i=4, t=PACK),
-                    squashed[b, half][:, :, u * PIECE : (u + 1) * PIECE].rearrange("p t (c i) -> p c t i", i=4),
-                    gain_t[:, b, :].unsqueeze(1).unsqueeze(3).broadcast_to([P, PIECE // 4, PACK, 4]),
-                    ALU.mult,
-                )
-                pieces.append(rounded)
             for u in range(2):
                 quantise(pieces[u], hq[b, half], u * PIECE)
 
-        def second_stage(half, nt, on_scalar):
-            if nt not in y:
-                pair = ring.tile([P, 2 * S], F32, name="wide", bufs=2, align_bytes=64)
-                y[nt], y[nt + 1] = pair[:, 0:S], pair[:, S : 2 * S]
-            acc = bank()
-            for b in reversed(range(r_passes)):
-                codes, scales = hq[b, half]
-                nc.tensor.matmul_mx(
-                    out=acc[:],
-                    lhsT=w2_w[:, b, 2 * P * nt : 2 * P * (nt + 1)].bitcast(FP4X4),
-                    lhsT_scale=w2_s[:, b, P * nt : P * (nt + 1)],
-                    rhs=codes[:].bitcast(FP8X4),
-                    rhs_scale=scales[:],
-                    start=(b == r_passes - 1),
-                    stop=(b == 0),
+        def make_h_on_vector(b, half):
+            factor = gain_t[:, b, :].unsqueeze(1).unsqueeze(3).broadcast_to([P, PIECE // LINE, PACK, LINE])
+            pieces = []
+            for u in range(2):
+                rounded = share([P, PIECE * PACK], BF16, "by_vector", 2)
+                nc.vector.tensor_tensor(as_words(rounded[:]), by_lines(squashed[b, half], u), factor, ALU.mult)
+                pieces.append(rounded[:])
+            quantise_h(b, half, pieces)
+
+        def scale_h_on_scalar(b):
+            scaled[b] = share([P, PACK, BANK], BF16, f"squashed{b}0", 1)
+            for t in range(PACK):
+                nc.scalar.activation(
+                    scaled[b][:, t, :], squashed[b, 1][:, t, :], ACT.Copy, scale=gain_t[:, b, t : t + 1]
                 )
-            if on_scalar:
+
+        def interleave_h(b, pieces):
+            for u in range(2):
+                nc.vector.tensor_copy(as_words(pieces[u]), by_lines(scaled[b], u))
+            quantise_h(b, 1, pieces)
+
+        def late_buffer(a):
+            return share([P, PIECE * PACK], BF16, f"late{a}", 1)
+
+        def round_w3(a, part, engine):
+            w3r[a, part] = late_buffer(a)
+            round_on(
+                engine,
+                w3r[a, part][:].rearrange("p (c l i) -> p c i l", l=LINE, i=PACK),
+                w3_raw[a, part][:].rearrange("p i (c l) -> p c i l", l=LINE),
+            )
+
+        def quantise_w3(a, part):
+            w3q[a, part] = mx_tiles(PIECE, f"w3q{a}{part}")
+            quantise(w3r[a, part][:], w3q[a, part], 0)
+
+        def second_stage(half):
+            for nt in range(n_tiles):
+                if nt not in y:
+                    pair = share([P, 2 * S], F32, "wide", 2)
+                    y[nt], y[nt + 1] = pair[:, 0:S], pair[:, S : 2 * S]
+                acc = bank()
+                for b in reversed(range(r_passes)):
+                    codes, scales = hq[b, half]
+                    nc.tensor.matmul_mx(
+                        out=acc[:],
+                        lhsT=w2_w[:, b, 2 * P * nt : 2 * P * (nt + 1)].bitcast(FP4X4),
+                        lhsT_scale=w2_s[:, b, P * nt : P * (nt + 1)],
+                        rhs=codes[:].bitcast(FP8X4),
+                        rhs_scale=scales[:],
+                        start=(b == r_passes - 1),
+                        stop=(b == 0),
+                    )
                 nc.scalar.activation(y[nt][:, half * BANK : (half + 1) * BANK], acc[:], ACT.Copy)
-            else:
-                nc.vector.tensor_copy(y[nt][:, half * BANK : (half + 1) * BANK], acc[:])
 
-        sums = {}
+        grown = [keep([P, N], F32, f"grown{jt}") for jt in range(j_tiles)]
+        wave = {(part, g): keep([P, BANK], F32, f"wave{part}{g}") for part in range(W3_PARTS) for g in range(2)}
 
-        def exp_part(jt):
-            acc = bank()
+        def note_product(dst, jt, weight):
             cols = slice(jt * P, (jt + 1) * P)
             for a in range(m_passes):
+                codes, scales = weight(a)
                 nc.tensor.matmul_mx(
-                    out=acc[:],
+                    out=dst,
                     lhsT=v2_w[a][:, cols].bitcast(FP8X4),
                     lhsT_scale=v2_s[4 * a : P, cols],
-                    rhs=w4_w[:, a, :].bitcast(FP8X4),
-                    rhs_scale=w4_s[4 * a : P, :],
+                    rhs=codes.bitcast(FP8X4),
+                    rhs_scale=scales,
                     start=(a == 0),
                     stop=(a == m_passes - 1),
                 )
-            nc.scalar.activation(grown[jt][:], acc[:], ACT.Exp)
 
-        def sine_pair(pair):
-            part = pair[0] // 2
-            for slot in pair:
+        def exponentials():
+            for jt in range(j_tiles):
                 acc = bank()
-                for side in range(2):
-                    jt = 2 * (slot % 2) + side
-                    cols = slice(jt * P, (jt + 1) * P)
-                    for a in range(m_passes):
-                        codes, scales = w3q[a, part]
-                        nc.tensor.matmul_mx(
-                            out=acc[:, side * W3_COLS : (side + 1) * W3_COLS],
-                            lhsT=v2_w[a][:, cols].bitcast(FP8X4),
-                            lhsT_scale=v2_s[4 * a : P, cols],
-                            rhs=codes[:].bitcast(FP8X4),
-                            rhs_scale=scales[:],
-                            start=(a == 0),
-                            stop=(a == m_passes - 1),
-                        )
-                nc.scalar.activation(wave[slot][:], acc[:], ACT.Sin, bias=eighth_pi[:], scale=-0.25)
-            for slot in pair:
-                nc.scalar.activation(wave[slot][:], wave[slot][:], ACT.Square)
-            for slot in pair:
+                note_product(acc[:], jt, lambda a: (w4_w[:, a, :], w4_s[4 * a : P, :]))
+                nc.scalar.activation(grown[jt][:], acc[:], ACT.Exp)
+
+        def sines(part):
+            for g in range(2):
+                acc = bank()
+                for s in range(2):
+                    note_product(
+                        acc[:, s * PIECE : (s + 1) * PIECE],
+                        2 * g + s,
+                        lambda a: (w3q[a, part][0][:], w3q[a, part][1][:]),
+                    )
+                nc.scalar.activation(wave[part, g][:], acc[:], ACT.Sin, bias=eighth_pi[:], scale=-0.25)
+
+        def squares(part):
+            for g in range(2):
+                nc.scalar.activation(wave[part, g][:], wave[part, g][:], ACT.Square)
+            for g in range(2):
                 nc.scalar.activation(
-                    wave[slot][:], wave[slot][:], ACT.Square, bias=root_two[:], scale=-2.0 * math.sqrt(2.0)
+                    wave[part, g][:], wave[part, g][:], ACT.Square, bias=root_two[:], scale=-2.0 * math.sqrt(2.0)
                 )
 
-        def note_sum(nt):
+        def turn_and_add(nt, jt, src, start, stop):
+            dst = sums[nt][:, jt * P : (jt + 1) * P]
+            nc.tensor.matmul(dst, src, identity[:], is_transpose=True, start=start, stop=stop)
+
+        def open_sum(nt):
             sums[nt] = bank()
-            part, first = divmod(nt * P, W3_COLS)
-            for jt in range(NOTES // P):
-                dst = sums[nt][:, jt * P : (jt + 1) * P]
-                at = (jt % 2) * W3_COLS + first
-                nc.tensor.matmul(
-                    dst, grown[jt][:, nt * P : (nt + 1) * P], identity[:], is_transpose=True, start=True, stop=False
-                )
-                nc.tensor.matmul(
-                    dst, wave[2 * part + jt // 2][:, at : at + P], identity[:], is_transpose=True, start=False, stop=True
-                )
+            for jt in range(j_tiles):
+                turn_and_add(nt, jt, grown[jt][:, nt * P : (nt + 1) * P], jt == 0, False)
 
-        def pick(nt):
-            picked_y[nt] = gather(y[nt], pos_t[:], F32, f"picked_y{nt}")
+        def close_sum(nt):
+            part, first = divmod(nt * P, PIECE)
+            for jt in range(j_tiles):
+                at = (jt % 2) * PIECE + first
+                turn_and_add(nt, jt, wave[part, jt // 2][:, at : at + P], False, jt == j_tiles - 1)
 
         def finish(nt):
             nc.vector.scalar_tensor_tensor(picked_y[nt][:], sums[nt][:], -1.0, picked_y[nt][:], ALU.add, ALU.max)
             nc.sync.dma_start(out=out[nt * P : (nt + 1) * P, :], in_=picked_y[nt][:])
 
-        def load_w3(part, a):
-            w3raw[a, part] = load_rows(w3[a * PASS : (a + 1) * PASS, part * W3_COLS : (part + 1) * W3_COLS])
+        def columns(dtype):
+            return share([P, BANK], dtype, "columns", k_passes * halves)
 
-        def cast_w3(part, a, eng):
-            w3r[a, part] = round_w3(w3raw[a, part], eng)
-
-        def quant_w3(part, a):
-            w3q[a, part] = mx_tiles(W3_COLS, f"w3q{a}{part}")
-            quantise(w3r[a, part], w3q[a, part], 0)
-
-
-        identity = keep([P, P], F32, "identity")
-        make_identity(nc, identity[:])
-        raw = load_rows(w1_rows(0, 0))
+        raw = load_w1(0, 0)
         nc.sync.dma_start(offs_t[:], offs)
         load_words(tab_w[0], tab_words[0])
-        make_w1(raw, 0, 0, "SS")
-
+        make_w1(raw, 0, 0, nc.scalar, "by_scalar")
+        nc.sync.dma_start(out=vector_rows[0:r_passes, :], in_=b1.rearrange("(b c) -> b c", c=PASS))
+        nc.sync.dma_start(out=vector_rows[r_passes : 2 * r_passes, :], in_=gain.rearrange("(b c) -> b c", c=PASS))
+        turned = bank()
+        for t in range(PACK):
+            nc.tensor.transpose(turned[:, t * P : (t + 1) * P], vector_rows[:, t:PASS:PACK], identity[:])
+        nc.scalar.copy(per_row[:], turned[:].rearrange("p (t k) -> p k t", t=PACK)[:, 0 : 2 * r_passes, :])
         load_packed_scales(tab_s, tab_scales)
-        raw = load_rows(w1_rows(1, 0))
+        raw = load_w1(1, 0)
         load_words(tab_w[1], tab_words[1])
-        nc.sync.dma_start(out=b1_t[:], in_=b1.rearrange("(b p t) -> p b t", p=P, t=PACK))
-        nc.sync.dma_start(out=gain_t[:], in_=gain.rearrange("(b p t) -> p b t", p=P, t=PACK))
         for half in range(halves):
-            v_w[0, half] = gather(tab_w[0], visit_list(half), U32, f"v_w0{half}")
-        v_s = [gather(tab_s, visit_list(half), U8, f"v_s{half}") for half in range(halves)]
+            v_w[0, half] = gather(columns(U32), tab_w[0][:], visit_list(half))
+        v_s = [gather(keep([P, BANK], U8, f"v_s{half}"), tab_s[:], visit_list(half)) for half in range(halves)]
+        make_w1(raw, 1, 0, nc.scalar, "by_scalar")
+        for half in range(halves):
+            v_w[1, half] = gather(columns(U32), tab_w[1][:], visit_list(half))
 
-        make_w1(raw, 1, 0, "SS")
-        for half in range(halves):
-            v_w[1, half] = gather(tab_w[1], visit_list(half), U32, f"v_w1{half}")
-        raws = [load_rows(w1_rows(a, 1)) for a in range(k_passes)]
+        w1_rest = [load_w1(a, 1) for a in range(k_passes)]
         nc.sync.dma_start(out=w2_w[:].bitcast(I32), in_=w2_words.rearrange("a p c -> p a c").bitcast(I32))
         nc.sync.dma_start(offs2_t[:], offs2)
         load_words(tab2_w[0], tab2_words[0])
@@ -327,48 +327,46 @@ def tile_list_dose_review_features_kernel(
         load_packed_scales(w4_s, w4_scales)
         nc.sync.dma_start(out=w4_w[:].bitcast(I32), in_=w4_words.rearrange("a p c i -> p a (c i)").bitcast(I32))
         nc.sync.dma_start(pos_t[:], pos1)
-        for a in range(m_passes):
-            load_w3(0, a)
-        for a in range(m_passes):
-            load_w3(1, a)
+        w3_raw = {(a, part): load_w3(a, part) for part in range(W3_PARTS) for a in range(m_passes)}
 
-        first_stage(0, 0)
-        make_w1(raws[0], 0, 1, "VV")
-        first_stage(0, 1)
-        make_w1(raws[1], 1, 1, "VV")
-        make_h(0, 0, "by_V")
-        first_stage(1, 0)
-        first_stage(1, 1)
-        make_h(1, 0, "by_V")
+        for half in range(halves):
+            first_stage(0, half)
+            make_w1(w1_rest[half], half, 1, nc.vector, "by_vector")
+        make_h_on_vector(0, 0)
+        for half in range(halves):
+            first_stage(1, half)
+        make_h_on_vector(1, 0)
+        scale_h_on_scalar(0)
+        second_stage(0)
+        scale_h_on_scalar(1)
+
+        v2_s = gather(keep([P, NOTES], U8, "v2_s"), tab2_s[:], offs2_t[:])
+        v2_w = [gather(keep([P, NOTES], U32, f"v2_w{a}"), tab2_w[a][:], offs2_t[:]) for a in range(m_passes)]
+        exponentials()
+        for a in range(m_passes):
+            round_w3(a, 0, nc.scalar if a == 0 else nc.vector)
+        after_notes = share([P, 2, PIECE * PACK], BF16, f"tab2_w{m_passes - 1}", 1)
+        interleave_h(0, [after_notes[:, u, :] for u in range(2)])
+        for a in range(m_passes):
+            quantise_w3(a, 0)
+        interleave_h(1, [late_buffer(1 + u)[:] for u in range(2)])
+        sines(0)
+        second_stage(1)
+        squares(0)
+        for a in range(m_passes):
+            round_w3(a, 1, nc.vector)
+        for a in range(m_passes):
+            quantise_w3(a, 1)
+        sines(1)
+        squares(1)
+
         for nt in range(n_tiles):
-            second_stage(0, nt, True)
-        v2_s = gather(tab2_s, offs2_t[:], U8, "v2_s")
-        v2_w = [gather(tab2_w[a], offs2_t[:], U32, f"v2_w{a}") for a in range(m_passes)]
-        for nt in range(n_tiles):
-            exp_part(nt)
-        for a in range(m_passes):
-            cast_w3(0, a, "SVV"[a])
-        make_h(0, 1, "tab2_w2")
-        for a in range(m_passes):
-            quant_w3(0, a)
-        make_h(1, 1, "rounded3")
-        sine_pair((0, 1))
-        for nt in range(n_tiles):
-            second_stage(1, nt, True)
-        for a in range(m_passes):
-            cast_w3(1, a, "VVV"[a])
-        for a in range(m_passes):
-            quant_w3(1, a)
-        sine_pair((2, 3))
-        note_sum(0)
-        note_sum(1)
-        pick(0)
-        pick(1)
-        finish(0)
-        finish(1)
-        pick(2)
-        pick(3)
-        note_sum(2)
-        note_sum(3)
-        finish(2)
-        finish(3)
+            picked_y[nt] = gather(columns(F32), y[nt], pos_t[:])
+        for part in range(W3_PARTS):
+            tiles = range(part * n_tiles // W3_PARTS, (part + 1) * n_tiles // W3_PARTS)
+            for nt in tiles:
+                open_sum(nt)
+            for nt in tiles:
+                close_sum(nt)
+            for nt in tiles:
+                finish(nt)

import math
from contextlib import ExitStack

import concourse.mybir as mybir
from concourse.masks import make_identity

K, T, S, H, K2, T3, NOTES, N = 1024, 4096, 1024, 1024, 1536, 2048, 512, 512
FLOPS = 2 * K * H * S + 2 * H * N * S + 2 * 2 * K2 * N * NOTES

F32 = mybir.dt.float32
BF16 = mybir.dt.bfloat16
I32 = mybir.dt.int32
U32 = mybir.dt.uint32
U16 = mybir.dt.uint16
U8 = mybir.dt.uint8
FP8X4 = mybir.dt.float8_e4m3fn_x4
FP4X4 = mybir.dt.float4_e2m1fn_x4
ACT = mybir.ActivationFunctionType
ALU = mybir.AluOpType

P = 128
PACK = 4
PASS = P * PACK
BANK = 512
QUADS = 4
LINE = 4
PIECE = BANK // 2
W3_PARTS = N // PIECE


def tile_list_dose_review_features_kernel(
    tc, tab_words, tab_scales, tab2_words, tab2_scales, w1, b1, gain, w2_words, w2_scales,
    w3, w4_words, w4_scales, offs, offs2, pos1, out,
):
    nc = tc.nc
    k_passes, r_passes, m_passes = K // PASS, H // PASS, K2 // PASS
    halves, n_tiles, j_tiles = S // BANK, N // P, NOTES // P

    with ExitStack() as ctx:
        held = ctx.enter_context(tc.tile_pool(name="held", bufs=1))
        ring = ctx.enter_context(tc.tile_pool(name="ring", bufs=1))
        psum = ctx.enter_context(tc.psum_pool(name="psum", bufs=8))

        def keep(shape, dtype, name):
            return held.tile(shape, dtype, name=name, align_bytes=64)

        def share(shape, dtype, tag, bufs):
            return ring.tile(shape, dtype, name=tag, bufs=bufs, align_bytes=64)

        def bank():
            return psum.tile([P, BANK], F32, name="bank")

        offs_t = held.tile([P, S // 16], U16, name="offs_t")
        offs2_t = held.tile([P, NOTES // 16], U16, name="offs2_t")
        pos_t = held.tile([P, NOTES // 16], U16, name="pos_t")
        vector_rows = keep([P, PASS], F32, "vector_rows")
        per_row = keep([P, 2 * r_passes, PACK], F32, "per_row")
        b1_t, gain_t = per_row[:, 0:r_passes, :], per_row[:, r_passes : 2 * r_passes, :]
        tab_w = [share([P, T], U32, "wide", 2) for a in range(k_passes)]
        tab_s = keep([P, T], U8, "tab_s")
        tab2_w = [share([P, T3], U32, f"tab2_w{a}", 1) for a in range(m_passes)]
        tab2_s = keep([P, T3], U8, "tab2_s")
        w2_w = keep([P, r_passes, 2 * N], U8, "w2_w")
        w2_s = keep([P, r_passes, N], U8, "w2_s")
        w4_w = keep([P, m_passes, N], U32, "w4_w")
        w4_s = keep([P, N], U8, "w4_s")

        nc.vector.memset(tab_s[:].bitcast(I32), 0)
        nc.vector.memset(vector_rows[:], 0.0)
        nc.vector.memset(tab2_s[:].bitcast(I32), 0)
        nc.vector.memset(w2_s[:].rearrange("p a n -> p (a n)").bitcast(I32), 0)
        nc.vector.memset(w4_s[:].bitcast(I32), 0)

        one = keep([P, 1], F32, "one")
        eighth_pi = keep([P, 1], F32, "eighth_pi")
        root_two = keep([P, 1], F32, "root_two")
        nc.vector.memset(one[:], 1.0)
        nc.vector.tensor_scalar(eighth_pi[:], one[:], math.pi / 8, None, ALU.mult)
        nc.vector.tensor_scalar(root_two[:], one[:], math.sqrt(2.0), None, ALU.mult)
        identity = keep([P, P], F32, "identity")
        make_identity(nc, identity[:])

        def load_words(tile, words):
            nc.sync.dma_start(out=tile[:].bitcast(I32), in_=words.rearrange("p t i -> p (t i)").bitcast(I32))

        def load_packed_scales(tile, scales):
            rows = 4 * scales.shape[0]
            for q in range(QUADS):
                nc.sync.dma_start(
                    out=tile[32 * q : 32 * q + rows, :].bitcast(I32),
                    in_=scales[:, 4 * q : 4 * q + 4, :].bitcast(I32),
                )

        def load_w2_scales():
            for q in range(QUADS):
                nc.sync.dma_start(
                    out=w2_s[32 * q : 32 * q + 4, :, :].bitcast(I32),
                    in_=w2_scales[:, 4 * q : 4 * q + 4, :].rearrange("a r n -> r a n").bitcast(I32),
                )

        def load_rows(rows, tag, bufs):
            raw = ring.tile([P, PACK, rows.shape[1]], F32, name=tag, bufs=bufs)
            nc.sync.dma_start(out=raw[:], in_=rows.rearrange("(p i) c -> p i c", i=PACK))
            return raw

        def load_w1(a, b):
            rows = w1[a * PASS : (a + 1) * PASS, b * PASS : (b + 1) * PASS]
            return load_rows(rows, "w1_raw", k_passes * r_passes)

        def load_w3(a, part):
            rows = w3[a * PASS : (a + 1) * PASS, part * PIECE : (part + 1) * PIECE]
            return load_rows(rows, "w3_raw", m_passes * W3_PARTS)

        def mx_tiles(words, name):
            return keep([P, words], U32, name + "_w"), keep([P, words], U8, name + "_s")

        def round_on(engine, dst, src):
            if engine is nc.scalar:
                nc.scalar.activation(dst, src, ACT.Copy)
            else:
                nc.vector.tensor_copy(dst, src)

        def quantise(rounded, target, first):
            codes, scales = target
            cols = slice(first, first + PIECE)
            nc.vector.quantize_mx(out=codes[:, cols].bitcast(FP8X4), scales=scales[:, cols], in_=rounded)

        def gather(picked, window, offsets):
            nc.vector.tensor_copy(picked[:], window.indirect(offsets))
            return picked

        def visit_list(half):
            return offs_t[:, half * (BANK // 16) : (half + 1) * (BANK // 16)]

        w1q, v_w, squashed, scaled, hq, w3r, w3q, y, sums, picked_y = {}, {}, {}, {}, {}, {}, {}, {}, {}, {}

        def make_w1(raw, a, b, engine, tag):
            w1q[a, b] = [mx_tiles(PIECE, f"w1q{a}{b}{u}") for u in range(2)]
            pieces = []
            for u in range(2):
                rounded = share([P, PIECE * PACK], BF16, tag, 2)
                round_on(
                    engine,
                    rounded[:].rearrange("p (t m i) -> p m i t", t=2, i=PACK),
                    raw[:].rearrange("p i (m t) -> p m i t", t=PACK)[:, :, :, 2 * u : 2 * u + 2],
                )
                pieces.append(rounded)
            for u in range(2):
                quantise(pieces[u][:], w1q[a, b][u], 0)

        def first_stage(b, half):
            squashed[b, half] = share([P, PACK, BANK], F32, f"squashed{b}{half}", 1)
            for t in range(PACK):
                acc = bank()
                cols = slice((t % 2) * P, (t % 2 + 1) * P)
                for a in range(k_passes):
                    codes, scales = w1q[a, b][t // 2]
                    nc.tensor.matmul_mx(
                        out=acc[:],
                        lhsT=codes[:, cols].bitcast(FP8X4),
                        lhsT_scale=scales[:, cols],
                        rhs=v_w[a, half][:].bitcast(FP8X4),
                        rhs_scale=v_s[half][4 * a : P, :],
                        start=(a == 0),
                        stop=(a == k_passes - 1),
                    )
                nc.scalar.activation(squashed[b, half][:, t, :], acc[:], ACT.Tanh, bias=b1_t[:, b, t : t + 1])

        def by_lines(planes, u):
            return planes[:, :, u * PIECE : (u + 1) * PIECE].rearrange("p t (c l) -> p c t l", l=LINE)

        def as_words(rounded):
            return rounded.rearrange("p (c l t) -> p c t l", l=LINE, t=PACK)

        def quantise_h(b, half, pieces):
            hq[b, half] = mx_tiles(BANK, f"hq{b}{half}")
            for u in range(2):
                quantise(pieces[u], hq[b, half], u * PIECE)

        def make_h_on_vector(b, half):
            factor = gain_t[:, b, :].unsqueeze(1).unsqueeze(3).broadcast_to([P, PIECE // LINE, PACK, LINE])
            pieces = []
            for u in range(2):
                rounded = share([P, PIECE * PACK], BF16, "by_vector", 2)
                nc.vector.tensor_tensor(as_words(rounded[:]), by_lines(squashed[b, half], u), factor, ALU.mult)
                pieces.append(rounded[:])
            quantise_h(b, half, pieces)

        def scale_h_on_scalar(b):
            scaled[b] = share([P, PACK, BANK], BF16, f"squashed{b}0", 1)
            for t in range(PACK):
                nc.scalar.activation(
                    scaled[b][:, t, :], squashed[b, 1][:, t, :], ACT.Copy, scale=gain_t[:, b, t : t + 1]
                )

        def interleave_h(b, pieces):
            for u in range(2):
                nc.vector.tensor_copy(as_words(pieces[u]), by_lines(scaled[b], u))
            quantise_h(b, 1, pieces)

        def late_buffer(a):
            return share([P, PIECE * PACK], BF16, f"late{a}", 1)

        def round_w3(a, part, engine):
            w3r[a, part] = late_buffer(a)
            round_on(
                engine,
                w3r[a, part][:].rearrange("p (c l i) -> p c i l", l=LINE, i=PACK),
                w3_raw[a, part][:].rearrange("p i (c l) -> p c i l", l=LINE),
            )

        def quantise_w3(a, part):
            w3q[a, part] = mx_tiles(PIECE, f"w3q{a}{part}")
            quantise(w3r[a, part][:], w3q[a, part], 0)

        def second_stage(half):
            for nt in range(n_tiles):
                if nt not in y:
                    pair = share([P, 2 * S], F32, "wide", 2)
                    y[nt], y[nt + 1] = pair[:, 0:S], pair[:, S : 2 * S]
                acc = bank()
                for b in reversed(range(r_passes)):
                    codes, scales = hq[b, half]
                    nc.tensor.matmul_mx(
                        out=acc[:],
                        lhsT=w2_w[:, b, 2 * P * nt : 2 * P * (nt + 1)].bitcast(FP4X4),
                        lhsT_scale=w2_s[:, b, P * nt : P * (nt + 1)],
                        rhs=codes[:].bitcast(FP8X4),
                        rhs_scale=scales[:],
                        start=(b == r_passes - 1),
                        stop=(b == 0),
                    )
                nc.scalar.activation(y[nt][:, half * BANK : (half + 1) * BANK], acc[:], ACT.Copy)

        grown = [keep([P, N], F32, f"grown{jt}") for jt in range(j_tiles)]
        wave = {(part, g): keep([P, BANK], F32, f"wave{part}{g}") for part in range(W3_PARTS) for g in range(2)}

        def note_product(dst, jt, weight):
            cols = slice(jt * P, (jt + 1) * P)
            for a in range(m_passes):
                codes, scales = weight(a)
                nc.tensor.matmul_mx(
                    out=dst,
                    lhsT=v2_w[a][:, cols].bitcast(FP8X4),
                    lhsT_scale=v2_s[4 * a : P, cols],
                    rhs=codes.bitcast(FP8X4),
                    rhs_scale=scales,
                    start=(a == 0),
                    stop=(a == m_passes - 1),
                )

        def exponentials():
            for jt in range(j_tiles):
                acc = bank()
                note_product(acc[:], jt, lambda a: (w4_w[:, a, :], w4_s[4 * a : P, :]))
                nc.scalar.activation(grown[jt][:], acc[:], ACT.Exp)

        def sines(part):
            for g in range(2):
                acc = bank()
                for s in range(2):
                    note_product(
                        acc[:, s * PIECE : (s + 1) * PIECE],
                        2 * g + s,
                        lambda a: (w3q[a, part][0][:], w3q[a, part][1][:]),
                    )
                nc.scalar.activation(wave[part, g][:], acc[:], ACT.Sin, bias=eighth_pi[:], scale=-0.25)

        def squares(part):
            for g in range(2):
                nc.scalar.activation(wave[part, g][:], wave[part, g][:], ACT.Square)
            for g in range(2):
                nc.scalar.activation(
                    wave[part, g][:], wave[part, g][:], ACT.Square, bias=root_two[:], scale=-2.0 * math.sqrt(2.0)
                )

        def turn_and_add(nt, jt, src, start, stop):
            dst = sums[nt][:, jt * P : (jt + 1) * P]
            nc.tensor.matmul(dst, src, identity[:], is_transpose=True, start=start, stop=stop)

        def open_sum(nt):
            sums[nt] = bank()
            for jt in range(j_tiles):
                turn_and_add(nt, jt, grown[jt][:, nt * P : (nt + 1) * P], jt == 0, False)

        def close_sum(nt):
            part, first = divmod(nt * P, PIECE)
            for jt in range(j_tiles):
                at = (jt % 2) * PIECE + first
                turn_and_add(nt, jt, wave[part, jt // 2][:, at : at + P], False, jt == j_tiles - 1)

        def finish(nt):
            nc.vector.scalar_tensor_tensor(picked_y[nt][:], sums[nt][:], -1.0, picked_y[nt][:], ALU.add, ALU.max)
            nc.sync.dma_start(out=out[nt * P : (nt + 1) * P, :], in_=picked_y[nt][:])

        def columns(dtype):
            return share([P, BANK], dtype, "columns", k_passes * halves)

        raw = load_w1(0, 0)
        nc.sync.dma_start(offs_t[:], offs)
        load_words(tab_w[0], tab_words[0])
        make_w1(raw, 0, 0, nc.scalar, "by_scalar")
        nc.sync.dma_start(out=vector_rows[0:r_passes, :], in_=b1.rearrange("(b c) -> b c", c=PASS))
        nc.sync.dma_start(out=vector_rows[r_passes : 2 * r_passes, :], in_=gain.rearrange("(b c) -> b c", c=PASS))
        turned = bank()
        for t in range(PACK):
            nc.tensor.transpose(turned[:, t * P : (t + 1) * P], vector_rows[:, t:PASS:PACK], identity[:])
        nc.scalar.copy(per_row[:], turned[:].rearrange("p (t k) -> p k t", t=PACK)[:, 0 : 2 * r_passes, :])
        load_packed_scales(tab_s, tab_scales)
        raw = load_w1(1, 0)
        load_words(tab_w[1], tab_words[1])
        for half in range(halves):
            v_w[0, half] = gather(columns(U32), tab_w[0][:], visit_list(half))
        v_s = [gather(keep([P, BANK], U8, f"v_s{half}"), tab_s[:], visit_list(half)) for half in range(halves)]
        make_w1(raw, 1, 0, nc.scalar, "by_scalar")
        for half in range(halves):
            v_w[1, half] = gather(columns(U32), tab_w[1][:], visit_list(half))

        w1_rest = [load_w1(a, 1) for a in range(k_passes)]
        nc.sync.dma_start(out=w2_w[:].bitcast(I32), in_=w2_words.rearrange("a p c -> p a c").bitcast(I32))
        nc.sync.dma_start(offs2_t[:], offs2)
        load_words(tab2_w[0], tab2_words[0])
        load_packed_scales(tab2_s, tab2_scales)
        load_words(tab2_w[1], tab2_words[1])
        load_w2_scales()
        load_words(tab2_w[2], tab2_words[2])
        load_packed_scales(w4_s, w4_scales)
        nc.sync.dma_start(out=w4_w[:].bitcast(I32), in_=w4_words.rearrange("a p c i -> p a (c i)").bitcast(I32))
        nc.sync.dma_start(pos_t[:], pos1)
        w3_raw = {(a, part): load_w3(a, part) for part in range(W3_PARTS) for a in range(m_passes)}

        for half in range(halves):
            first_stage(0, half)
            make_w1(w1_rest[half], half, 1, nc.vector, "by_vector")
        make_h_on_vector(0, 0)
        for half in range(halves):
            first_stage(1, half)
        make_h_on_vector(1, 0)
        scale_h_on_scalar(0)
        second_stage(0)
        scale_h_on_scalar(1)

        v2_s = gather(keep([P, NOTES], U8, "v2_s"), tab2_s[:], offs2_t[:])
        v2_w = [gather(keep([P, NOTES], U32, f"v2_w{a}"), tab2_w[a][:], offs2_t[:]) for a in range(m_passes)]
        exponentials()
        for a in range(m_passes):
            round_w3(a, 0, nc.scalar if a == 0 else nc.vector)
        after_notes = share([P, 2, PIECE * PACK], BF16, f"tab2_w{m_passes - 1}", 1)
        interleave_h(0, [after_notes[:, u, :] for u in range(2)])
        for a in range(m_passes):
            quantise_w3(a, 0)
        interleave_h(1, [late_buffer(1 + u)[:] for u in range(2)])
        sines(0)
        second_stage(1)
        squares(0)
        for a in range(m_passes):
            round_w3(a, 1, nc.vector)
        for a in range(m_passes):
            quantise_w3(a, 1)
        sines(1)
        squares(1)

        for nt in range(n_tiles):
            picked_y[nt] = gather(columns(F32), y[nt], pos_t[:])
        for part in range(W3_PARTS):
            tiles = range(part * n_tiles // W3_PARTS, (part + 1) * n_tiles // W3_PARTS)
            for nt in tiles:
                open_sum(nt)
            for nt in tiles:
                close_sum(nt)
            for nt in tiles:
                finish(nt)
